import numpy as np
import ml_dtypes


def mxq(x, axis, fmt="e4m3"):
    dtype, down = {"e4m3": (ml_dtypes.float8_e4m3fn, 7), "e5m2": (ml_dtypes.float8_e5m2, 14)}[fmt]
    v = np.moveaxis(np.asarray(x, np.float32).astype(ml_dtypes.bfloat16).astype(np.float64), axis, -1)
    blocks = v.reshape(v.shape[:-1] + (-1, 32))
    amax = np.abs(blocks).max(-1, keepdims=True)
    byte = np.maximum(np.where(amax > 0, np.frexp(amax)[1] - 1 + 127, 0) - down, 1)
    scale = np.exp2(byte - 127.0)
    codes = (blocks / scale).astype(np.float32).astype(dtype).astype(np.float64)
    return np.moveaxis((codes * scale).reshape(v.shape), -1, axis)


WIDE = False


def mx_kscale(k):
    if not WIDE:
        return np.ones(k)
    levels = np.array([10, -10, 5, -5, 0])
    if k % 512:
        return np.exp2(np.random.permutation(np.resize(levels, k // 32))).repeat(32)
    a = np.empty((k // 512, 16))
    for p in range(k // 512):
        a[p, :8] = np.random.permutation(np.resize(levels, 8))
        for g in range(8):
            far = levels[np.abs(levels - a[p, g]) >= 10]
            a[p, g + 8] = far[np.random.randint(len(far))]
    return np.exp2(a.ravel()).repeat(32)


BF16 = ml_dtypes.bfloat16


def bf(x):
    return np.asarray(x, np.float32).astype(BF16)


def f64(x):
    return np.asarray(x).astype(np.float64)


E2M1 = np.array([0.0, 0.5, 1.0, 1.5, 2.0, 3.0, 4.0, 6.0, -0.0, -0.5, -1.0, -1.5, -2.0, -3.0, -4.0, -6.0])


def pack_weight(w, fmt):
    k, n = w.shape
    w = f64(bf(w)).reshape(k // 32, 32, n)
    amax = np.abs(w).max(1)
    if fmt == "e4m3":
        byte = np.frexp(amax)[1] - 1 + 127 - 7
    else:
        mant, ex = np.frexp(amax / 6.0)
        byte = np.where(mant > 0.5, ex, ex - 1) + 127
    byte = np.clip(np.where(amax > 0, byte, 1), 1, 254)
    scaled = (w * np.exp2(127.0 - byte)[:, None, :]).reshape(k, n).astype(np.float32)
    by_word = np.ascontiguousarray(scaled.reshape(k // 512, 128, 4, n).transpose(0, 1, 3, 2))
    if fmt == "e4m3":
        words = by_word.astype(ml_dtypes.float8_e4m3fn).view(np.uint8)
    else:
        c = by_word.astype(ml_dtypes.float4_e2m1fn).view(np.uint8) & 0xF
        words = c[..., 0::2] | (c[..., 1::2] << 4)
    return np.ascontiguousarray(words), np.ascontiguousarray(byte.astype(np.uint8).reshape(k // 512, 16, n))


def unpack_weight(words, scales, fmt):
    g, p, n, _ = words.shape
    if fmt == "e4m3":
        vals = np.ascontiguousarray(words).view(ml_dtypes.float8_e4m3fn).astype(np.float64)
    else:
        nib = np.empty((g, p, n, 4), np.uint8)
        nib[..., 0::2] = words & 0xF
        nib[..., 1::2] = words >> 4
        vals = E2M1[nib]
    vals = vals * np.repeat(np.exp2(scales.astype(np.float64) - 127.0), 8, axis=1)[..., None]
    return vals.transpose(0, 1, 3, 2).reshape(g * 512, n)
def pack4(w):
    words, scales = pack_weight(w, "e2m1")
    return words.reshape(words.shape[0], 128, -1), scales


def unpack4(words, scales):
    return unpack_weight(words.reshape(words.shape[0], 128, -1, 2), scales, "e2m1")


L, H, B, C, D = 1024, 512, 4, 1024, 1024


def setup_inputs():
    s = mx_kscale(L)
    t = mx_kscale(C)
    lag = np.random.standard_normal((L, H)) / np.sqrt(L) * s[:, None]
    x = np.random.standard_normal((L, B, C)) / s[:, None, None] * t
    w = np.random.standard_normal((C, D)) / np.sqrt(C) / t[:, None]
    lag_words, lag_scales = pack4(lag)
    x_words, x_scales = pack4(x.reshape(L, B * C))
    w_words, w_scales = pack_weight(w, "e4m3")
    return {"lag_words": lag_words, "lag_scales": lag_scales,
            "x_words": x_words, "x_scales": x_scales,
            "w_words": w_words, "w_scales": w_scales,
            "level": bf(0.5 * np.random.standard_normal((B, C)) * t),
            "bias": bf(0.3 * np.random.standard_normal(D))}


def reference(lag_words, lag_scales, x_words, x_scales, w_words, w_scales, level, bias):
    lag = unpack4(lag_words, lag_scales)
    x = unpack4(x_words, x_scales)
    w = unpack_weight(w_words, w_scales, "e4m3")
    m = (lag.T @ x).reshape(H, B, C)
    u = np.maximum(m + f64(level), 0.0)
    u = u.transpose(1, 0, 2).reshape(B * H, C)
    y = (mxq(u, 1, "e4m3") @ w) + f64(bias)
    return y.reshape(B, H, D)

@@ -1,0 +1,219 @@
+from contextlib import ExitStack
+
+import concourse.mybir as mybir
+
+L, H, B, C, D = 1024, 512, 4, 1024, 1024
+FLOPS = 2 * L * H * B * C + 2 * B * H * C * D
+
+F32 = mybir.dt.float32
+BF16 = mybir.dt.bfloat16
+I32 = mybir.dt.int32
+U32 = mybir.dt.uint32
+U8 = mybir.dt.uint8
+FP4X4 = mybir.dt.float4_e2m1fn_x4
+FP8X4 = mybir.dt.float8_e4m3fn_x4
+ADD = mybir.AluOpType.add
+RELU = mybir.ActivationFunctionType.Relu
+
+P = 128
+KG = L // 512
+CG = C // 512
+UNITS = B * CG
+NT = 512
+
+ORDER = """
+W:0.1 S:0 W:0.0 W:0.2 W:0.3 S:1 W:1 U:0 W:2 S:2 U:1 IS:1.256 U:2 S:3 W:3 IS:2.384 IV:1.256 IV:0.512 Q:1 U:3
+Q:0 S:4 W:4 IS:3.384 A:0.0.0 S:5 A:0.0.1 A:0.1.0 A:0.1.1 IG:2.128 A:0.2.0 W:5 A:0.2.1 A:0.3.0 A:0.3.1 Q:2
+IG:3.128 Q:3 U:4 S:6 U:5 W:6 IG:4.128 A:1.0.0 A:1.0.1 S:7 A:1.1.0 A:1.1.1 IS:5.384 A:1.2.0 W:7 A:1.2.1 A:1.3.0
+IS:4.384 IG:5.128 A:1.3.1 Q:5 U:6 U:7 IS:6.384 IS:7.384 Q:4 A:2.0.0 A:2.0.1 IG:6.128 IG:7.128 A:2.1.0 A:2.1.1
+H:2.2.0 Q:6 A:2.2.1 Q:7 H:2.3.0 A:2.3.1 H:3.0.0 A:3.0.1 H:3.1.0 A:3.1.1 A:3.2.0 A:3.2.1 A:3.3.0 A:3.3.1
+""".split()
+
+
+def tile_lag_channel_mixer_s4_kernel(
+    tc, lag_words, lag_scales, x_words, x_scales, w_words, w_scales, level, bias, out
+):
+    nc = tc.nc
+    with ExitStack() as ctx:
+        keep = ctx.enter_context(tc.tile_pool(name="keep", bufs=1))
+        work = ctx.enter_context(tc.tile_pool(name="work", bufs=3))
+        outs = ctx.enter_context(tc.tile_pool(name="outs", bufs=6))
+        psum = ctx.enter_context(tc.psum_pool(name="psum", bufs=8))
+        ctx.enter_context(tc.manual_schedule())
+
+        lag_w = keep.tile([P, KG, 2 * H], U8, align_bytes=64, name="lag_w")
+        lag_s = keep.tile([P, KG, H], U8, align_bytes=64, name="lag_s")
+        w_w = keep.tile([P, CG, 4 * D], U8, align_bytes=64, name="w_w")
+        w_s = keep.tile([P, CG, D], U8, align_bytes=64, name="w_s")
+        lvl = keep.tile([P, UNITS, 4], BF16, align_bytes=64, name="lvl")
+        bias_t = keep.tile([P, D], BF16, align_bytes=64, name="bias_t")
+        scratch = keep.tile([P, 1], F32, name="scratch")
+        x_raw = [keep.tile([P, KG, 1024], U8, align_bytes=64, name="x_raw%d" % u) for u in range(UNITS)]
+        x_st = [keep.tile([P, KG, 4, 256], U8, align_bytes=64, name="x_st%d" % u) for u in range(UNITS)]
+        xs_raw0 = keep.tile([P, KG, C], U8, align_bytes=64, name="xs_raw0")
+        xs_raw1 = keep.tile([P, KG, 3 * C], U8, align_bytes=64, name="xs_raw1")
+        xs_st = [keep.tile([P, KG, 4, P], U8, align_bytes=64, name="xs_st%d" % u) for u in range(UNITS)]
+
+        def load_x(u):
+            src = x_words[:, :, u * 1024 : (u + 1) * 1024].bitcast(I32)
+            nc.sync.dma_start(out=x_raw[u][:].bitcast(I32), in_=src.rearrange("k p n -> p k n"))
+
+        def load_scales(engine, dst, src, q):
+            rows = src[:, 4 * q : 4 * q + 4, :].bitcast(I32)
+            engine.dma_start(out=dst[32 * q : 32 * q + 4].bitcast(I32), in_=rows.rearrange("k r n -> r k n"))
+
+        nc.vector.memset(xs_raw0[:].rearrange("p k n -> p (k n)").bitcast(I32), 0)
+        nc.vector.memset(lag_s[:].rearrange("p k n -> p (k n)").bitcast(I32), 0)
+        load_x(0)
+        nc.scalar.dma_start(out=lag_w[:].bitcast(I32), in_=lag_words[:, :, :].bitcast(I32).rearrange("k p n -> p k n"))
+        for q in range(4):
+            load_scales(nc.sync, xs_raw0, x_scales[:, :, 0:C], q)
+        for q in range(2):
+            load_scales(nc.scalar, lag_s, lag_scales, q)
+        for q in range(2, 4):
+            load_scales(nc.gpsimd, lag_s, lag_scales, q)
+        nc.gpsimd.dma_start(out=lvl[:], in_=level.rearrange("b (g p t) -> p (b g) t", g=CG, t=4))
+        nc.gpsimd.memset(xs_raw1[:].rearrange("p k n -> p (k n)").bitcast(I32), 0)
+        nc.gpsimd.memset(w_s[:].rearrange("p k n -> p (k n)").bitcast(I32), 0)
+        nc.vector.memset(scratch[:], 0.0)
+        nc.scalar.activation(out=scratch[:], in_=scratch[:], func=RELU)
+        load_x(1)
+        load_x(2)
+        for q in range(4):
+            load_scales(nc.sync, xs_raw1, x_scales[:, :, C : 4 * C], q)
+        load_x(3)
+        for g in range(CG):
+            nc.sync.dma_start(
+                out=w_w[:, g, :].bitcast(I32),
+                in_=w_words[g].rearrange("p n t -> p (n t)").bitcast(I32),
+            )
+        for q in range(4):
+            load_scales(nc.sync, w_s, w_scales, q)
+        nc.sync.dma_start(out=bias_t[:], in_=bias.partition_broadcast(P))
+        for u in range(4, UNITS):
+            load_x(u)
+
+        def words(u):
+            nc.vector.tensor_copy(
+                out=x_st[u][:].rearrange("p k t (m b) -> p k t m b", b=2),
+                in_=x_raw[u][:].rearrange("p k (m t b) -> p k t m b", t=4, b=2),
+            )
+
+        def words_t(u, t):
+            nc.vector.tensor_copy(
+                out=x_st[u][:, :, t, :].rearrange("p k (m b) -> p k m b", b=2),
+                in_=x_raw[u][:].rearrange("p k (m t b) -> p k t m b", t=4, b=2)[:, :, t],
+            )
+
+        def scales(u):
+            b, g = divmod(u, CG)
+            raw = xs_raw0 if b == 0 else xs_raw1
+            c0 = 512 * u if b == 0 else 512 * (u - CG)
+            nc.vector.tensor_copy(
+                out=xs_st[u][:],
+                in_=raw[:, :, c0 : c0 + 512].rearrange("p k (m t) -> p k t m", t=4),
+            )
+
+        rows = {}
+        inter = {}
+        codes = {}
+        code_scales = {}
+
+        def stage1(u):
+            rows[u] = work.tile([P, 4, H], BF16, align_bytes=64, name="rows")
+            for t in range(4):
+                acc = psum.tile([P, NT], F32, name="acc")
+                for k in range(KG):
+                    nc.tensor.matmul_mx(
+                        out=acc[:],
+                        lhsT=x_st[u][:, k, t, :].bitcast(FP4X4),
+                        lhsT_scale=xs_st[u][:, k, t, :],
+                        rhs=lag_w[:, k, :].bitcast(FP4X4),
+                        rhs_scale=lag_s[:, k, :],
+                        start=(k == 0),
+                        stop=(k == KG - 1),
+                    )
+                nc.scalar.activation(
+                    out=rows[u][:, t, :], in_=acc[:], func=RELU, bias=lvl[:, u, t : t + 1]
+                )
+
+        def get_inter(u):
+            if u not in inter:
+                inter[u] = work.tile([P, H, 4], BF16, align_bytes=64, name="inter")
+            return inter[u]
+
+        filled = {}
+
+        def interleave(engine_copy, u, n):
+            n0 = filled.get(u, 0)
+            filled[u] = n0 + n
+            engine_copy(
+                out=get_inter(u)[:, n0 : n0 + n, :], in_=rows[u][:, :, n0 : n0 + n].rearrange("p t n -> p n t")
+            )
+
+        def interleave_g(out, in_):
+            nc.gpsimd.tensor_scalar(out=out, in0=in_, scalar1=1.0, scalar2=0.0, op0=mybir.AluOpType.mult, op1=ADD)
+
+        def quantise(u):
+            codes[u] = keep.tile([P, H], U32, align_bytes=64, name="codes%d" % u)
+            code_scales[u] = keep.tile([P, H], U8, align_bytes=64, name="cs%d" % u)
+            nc.vector.quantize_mx(
+                out=codes[u][:].bitcast(FP8X4),
+                scales=code_scales[u][:],
+                in_=inter[u][:].rearrange("p n t -> p (n t)"),
+            )
+
+        y_tiles = {}
+
+        def stage2(b, m, d, helper):
+            if d == 0:
+                y_tiles[b, m] = outs.tile([P, D], F32, name="y")
+            y = y_tiles[b, m]
+            acc = psum.tile([P, NT], F32, name="acc")
+            for g in range(CG):
+                u = b * CG + g
+                nc.tensor.matmul_mx(
+                    out=acc[:],
+                    lhsT=codes[u][:, m * P : (m + 1) * P].bitcast(FP8X4),
+                    lhsT_scale=code_scales[u][:, m * P : (m + 1) * P],
+                    rhs=w_w[:, g, 4 * d * NT : 4 * (d + 1) * NT].bitcast(FP8X4),
+                    rhs_scale=w_s[:, g, d * NT : (d + 1) * NT],
+                    start=(g == 0),
+                    stop=(g == CG - 1),
+                )
+            cols = slice(d * NT, (d + 1) * NT)
+            if helper:
+                nc.scalar.copy(out=y[:, cols], in_=acc[:])
+                nc.gpsimd.tensor_tensor(out=y[:, cols], in0=y[:, cols], in1=bias_t[:, cols], op=ADD)
+            else:
+                nc.vector.tensor_tensor(out=y[:, cols], in0=acc[:], in1=bias_t[:, cols], op=ADD)
+            if (b, m) == (B - 1, H // P - 1):
+                engine = nc.sync if d == 0 else nc.scalar
+                engine.dma_start(out=out[b, m * P : (m + 1) * P, cols], in_=y[:, cols])
+            elif d == D // NT - 1:
+                nc.sync.dma_start(out=out[b, m * P : (m + 1) * P, :], in_=y[:])
+
+        for token in ORDER:
+            kind, rest = token.split(":")
+            a = [int(v) for v in rest.split(".")]
+            if kind == "W":
+                if len(a) == 1:
+                    words(a[0])
+                else:
+                    words_t(a[0], a[1])
+            elif kind == "S":
+                scales(a[0])
+            elif kind == "U":
+                stage1(a[0])
+            elif kind == "IV":
+                interleave(nc.vector.tensor_copy, a[0], a[1])
+            elif kind == "IS":
+                interleave(nc.scalar.copy, a[0], a[1])
+            elif kind == "IG":
+                interleave(interleave_g, a[0], a[1])
+            elif kind == "Q":
+                quantise(a[0])
+            elif kind == "A":
+                stage2(a[0], a[1], a[2], False)
+            else:
+                stage2(a[0], a[1], a[2], True)

@@ -22,12 +22,13 @@ UNITS = B * CG
 NT = 512
 
 ORDER = """
-W:0.1 S:0 W:0.0 W:0.2 W:0.3 S:1 W:1 U:0 W:2 S:2 U:1 IS:1.256 U:2 S:3 W:3 IS:2.384 IV:1.256 IV:0.512 Q:1 U:3
-Q:0 S:4 W:4 IS:3.384 A:0.0.0 S:5 A:0.0.1 A:0.1.0 A:0.1.1 IG:2.128 A:0.2.0 W:5 A:0.2.1 A:0.3.0 A:0.3.1 Q:2
-IG:3.128 Q:3 U:4 S:6 U:5 W:6 IG:4.128 A:1.0.0 A:1.0.1 S:7 A:1.1.0 A:1.1.1 IS:5.384 A:1.2.0 W:7 A:1.2.1 A:1.3.0
-IS:4.384 IG:5.128 A:1.3.1 Q:5 U:6 U:7 IS:6.384 IS:7.384 Q:4 A:2.0.0 A:2.0.1 IG:6.128 IG:7.128 A:2.1.0 A:2.1.1
-H:2.2.0 Q:6 A:2.2.1 Q:7 H:2.3.0 A:2.3.1 H:3.0.0 A:3.0.1 H:3.1.0 A:3.1.1 A:3.2.0 A:3.2.1 A:3.3.0 A:3.3.1
+W:0.0 S:0 W:0.1 W:0.2 W:0.3 U:0 W:1 S:1 U:1 W:2 S:2 IV:0.512 S:3 IV:1.256 IS:1.256 Q:0 Q:1 W:3 U:2 IS:2.512
+H:0 W:4 SP:0 E:0.0 E:0.1 E:0.2 E:0.3 Q:2 U:3 IS:3.384 H:1 E:1.0 E:1.1 IV:3.128 E:1.2 Q:3 E:1.3 W:5 U:4
+IS:4.512 H:2 W:6 E:2.0 E:2.1 E:2.2 E:2.3 Q:4 U:5 IS:5.384 H:3 E:3.0 E:3.1 IV:5.128 E:3.2 Q:5 E:3.3 W:7 U:6
+IS:6.512 H:4 E:4.0 E:4.1 E:4.2 E:4.3 Q:6 U:7 IS:7.256 H:5 E:5.0 E:5.1 IV:7.256 E:5.2 Q:7 E:5.3 H:6 E:6.0 E:6.1
+E:6.2 E:6.3 H:7 E:7.0 E:7.1 E:7.2 E:7.3
 """.split()
+GROUP_FIRST = (0, 6)
 
 
 def tile_lag_channel_mixer_s4_kernel(
@@ -50,48 +51,67 @@ def tile_lag_channel_mixer_s4_kernel(
         scratch = keep.tile([P, 1], F32, name="scratch")
         x_raw = [keep.tile([P, KG, 1024], U8, align_bytes=64, name="x_raw%d" % u) for u in range(UNITS)]
         x_st = [keep.tile([P, KG, 4, 256], U8, align_bytes=64, name="x_st%d" % u) for u in range(UNITS)]
-        xs_raw0 = keep.tile([P, KG, C], U8, align_bytes=64, name="xs_raw0")
-        xs_raw1 = keep.tile([P, KG, 3 * C], U8, align_bytes=64, name="xs_raw1")
-        xs_st = [keep.tile([P, KG, 4, P], U8, align_bytes=64, name="xs_st%d" % u) for u in range(UNITS)]
+        xs_raw0 = keep.tile([P, KG, 2 * C], U8, align_bytes=64, name="xs_raw0")
+        xs_pk = keep.tile([P, 2 * C], U8, align_bytes=64, name="xs_pk")
+        pk_st = keep.tile([P, 2 * CG, 4, P], U8, align_bytes=64, name="pk_st")
+        pl1 = keep.tile([P, 2 * CG, 4, P], U8, align_bytes=64, name="pl1")
+        xs_st = [keep.tile([P, KG, CG, 4, P], U8, align_bytes=64, name="xs_st%d" % b) for b in range(2)]
+        codes = [keep.tile([P, H], U32, align_bytes=64, name="codes%d" % u) for u in range(UNITS)]
+        code_scales = [keep.tile([P, H], U8, align_bytes=64, name="cs%d" % u) for u in range(UNITS)]
 
-        def load_x(u):
+        def load_x(u, engine=nc.sync):
             src = x_words[:, :, u * 1024 : (u + 1) * 1024].bitcast(I32)
-            nc.sync.dma_start(out=x_raw[u][:].bitcast(I32), in_=src.rearrange("k p n -> p k n"))
+            engine.dma_start(out=x_raw[u][:].bitcast(I32), in_=src.rearrange("k p n -> p k n"))
 
         def load_scales(engine, dst, src, q):
             rows = src[:, 4 * q : 4 * q + 4, :].bitcast(I32)
             engine.dma_start(out=dst[32 * q : 32 * q + 4].bitcast(I32), in_=rows.rearrange("k r n -> r k n"))
 
-        nc.vector.memset(xs_raw0[:].rearrange("p k n -> p (k n)").bitcast(I32), 0)
         nc.vector.memset(lag_s[:].rearrange("p k n -> p (k n)").bitcast(I32), 0)
-        load_x(0)
-        nc.scalar.dma_start(out=lag_w[:].bitcast(I32), in_=lag_words[:, :, :].bitcast(I32).rearrange("k p n -> p k n"))
-        for q in range(4):
-            load_scales(nc.sync, xs_raw0, x_scales[:, :, 0:C], q)
-        for q in range(2):
-            load_scales(nc.scalar, lag_s, lag_scales, q)
-        for q in range(2, 4):
-            load_scales(nc.gpsimd, lag_s, lag_scales, q)
-        nc.gpsimd.dma_start(out=lvl[:], in_=level.rearrange("b (g p t) -> p (b g) t", g=CG, t=4))
-        nc.gpsimd.memset(xs_raw1[:].rearrange("p k n -> p (k n)").bitcast(I32), 0)
-        nc.gpsimd.memset(w_s[:].rearrange("p k n -> p (k n)").bitcast(I32), 0)
+        nc.vector.memset(xs_raw0[:].rearrange("p k n -> p (k n)").bitcast(I32), 0)
+        nc.vector.memset(codes[UNITS - 1][:], 0)
+        nc.vector.memset(code_scales[UNITS - 1][:].bitcast(I32), 0)
         nc.vector.memset(scratch[:], 0.0)
+        load_x(0)
+        nc.gpsimd.dma_start(out=lag_w[:].bitcast(I32), in_=lag_words[:, :, :].bitcast(I32).rearrange("k p n -> p k n"))
+        for q in range(4):
+            load_scales(nc.scalar if q < 3 else nc.gpsimd, lag_s, lag_scales, q)
+            load_scales(nc.sync, xs_raw0, x_scales[:, :, 0 : 2 * C], q)
+        nc.gpsimd.memset(xs_pk[:].bitcast(I32), 0)
+        nc.gpsimd.memset(pl1[:].rearrange("p a t m -> p (a t m)").bitcast(I32), 0)
+        nc.gpsimd.memset(w_s[:].rearrange("p k n -> p (k n)").bitcast(I32), 0)
         nc.scalar.activation(out=scratch[:], in_=scratch[:], func=RELU)
+        nc.scalar.dma_start(out=lvl[:], in_=level.rearrange("b (g p t) -> p (b g) t", g=CG, t=4))
         load_x(1)
         load_x(2)
         for q in range(4):
-            load_scales(nc.sync, xs_raw1, x_scales[:, :, C : 4 * C], q)
+            nc.sync.dma_start(
+                out=xs_pk[32 * q : 32 * q + 8, :].bitcast(I32),
+                in_=x_scales[:, 4 * q : 4 * q + 4, 2 * C : 4 * C].bitcast(I32),
+            )
+        for q in range(4):
+            load_scales(nc.sync, w_s, w_scales, q)
         load_x(3)
         for g in range(CG):
             nc.sync.dma_start(
                 out=w_w[:, g, :].bitcast(I32),
                 in_=w_words[g].rearrange("p n t -> p (n t)").bitcast(I32),
             )
-        for q in range(4):
-            load_scales(nc.sync, w_s, w_scales, q)
+        load_x(4)
         nc.sync.dma_start(out=bias_t[:], in_=bias.partition_broadcast(P))
-        for u in range(4, UNITS):
+        for u in range(5, UNITS):
             load_x(u)
+        warm = psum.tile([P, NT], F32, name="acc")
+        for i in range(6):
+            nc.tensor.matmul_mx(
+                out=warm[:],
+                lhsT=codes[UNITS - 1][:, 0:P].bitcast(FP8X4),
+                lhsT_scale=code_scales[UNITS - 1][:, 0:P],
+                rhs=codes[UNITS - 1][:].bitcast(FP8X4),
+                rhs_scale=code_scales[UNITS - 1][:],
+                start=True,
+                stop=True,
+            )
 
         def words(u):
             nc.vector.tensor_copy(
@@ -107,17 +127,24 @@ def tile_lag_channel_mixer_s4_kernel(
 
         def scales(u):
             b, g = divmod(u, CG)
-            raw = xs_raw0 if b == 0 else xs_raw1
-            c0 = 512 * u if b == 0 else 512 * (u - CG)
             nc.vector.tensor_copy(
-                out=xs_st[u][:],
-                in_=raw[:, :, c0 : c0 + 512].rearrange("p k (m t) -> p k t m", t=4),
+                out=xs_st[b][:, :, g], in_=xs_raw0[:, :, u * 512 : (u + 1) * 512].rearrange("p k (m t) -> p k t m", t=4)
             )
+
+        def scales_packed():
+            nc.vector.tensor_copy(out=pk_st[:], in_=xs_pk[:].rearrange("p (a m t) -> p a t m", t=4, m=P))
+            for q in range(4):
+                nc.sync.dma_start(
+                    out=pl1[32 * q : 32 * q + 4].bitcast(I32), in_=pk_st[32 * q + 4 : 32 * q + 8].bitcast(I32)
+                )
+
+        def x_scale(u, k, t):
+            if u < 2 * CG:
+                return xs_st[u // CG][:, k, u % CG, t, :]
+            return (pk_st, pl1)[k][:, u - 2 * CG, t, :]
 
         rows = {}
         inter = {}
-        codes = {}
-        code_scales = {}
 
         def stage1(u):
             rows[u] = work.tile([P, 4, H], BF16, align_bytes=64, name="rows")
@@ -127,7 +154,7 @@ def tile_lag_channel_mixer_s4_kernel(
                     nc.tensor.matmul_mx(
                         out=acc[:],
                         lhsT=x_st[u][:, k, t, :].bitcast(FP4X4),
-                        lhsT_scale=xs_st[u][:, k, t, :],
+                        lhsT_scale=x_scale(u, k, t),
                         rhs=lag_w[:, k, :].bitcast(FP4X4),
                         rhs_scale=lag_s[:, k, :],
                         start=(k == 0),
@@ -148,15 +175,14 @@ def tile_lag_channel_mixer_s4_kernel(
             n0 = filled.get(u, 0)
             filled[u] = n0 + n
             engine_copy(
-                out=get_inter(u)[:, n0 : n0 + n, :], in_=rows[u][:, :, n0 : n0 + n].rearrange("p t n -> p n t")
+                out=get_inter(u)[:, n0 : n0 + n, :].rearrange("p (c i) t -> p c t i", i=4),
+                in_=rows[u][:, :, n0 : n0 + n].rearrange("p t (c i) -> p c t i", i=4),
             )
 
         def interleave_g(out, in_):
             nc.gpsimd.tensor_scalar(out=out, in0=in_, scalar1=1.0, scalar2=0.0, op0=mybir.AluOpType.mult, op1=ADD)
 
         def quantise(u):
-            codes[u] = keep.tile([P, H], U32, align_bytes=64, name="codes%d" % u)
-            code_scales[u] = keep.tile([P, H], U8, align_bytes=64, name="cs%d" % u)
             nc.vector.quantize_mx(
                 out=codes[u][:].bitcast(FP8X4),
                 scales=code_scales[u][:],
@@ -164,34 +190,52 @@ def tile_lag_channel_mixer_s4_kernel(
             )
 
         y_tiles = {}
+        banks = {}
 
-        def stage2(b, m, d, helper):
+        def multiply(j, i, g, start, stop):
+            u = (j // 2) * CG + g
+            m, d = 2 * (j % 2) + i // 2, i % 2
+            if start:
+                banks[j, i] = psum.tile([P, NT], F32, name="acc")
+            nc.tensor.matmul_mx(
+                out=banks[j, i][:],
+                lhsT=codes[u][:, m * P : (m + 1) * P].bitcast(FP8X4),
+                lhsT_scale=code_scales[u][:, m * P : (m + 1) * P],
+                rhs=w_w[:, g, 4 * d * NT : 4 * (d + 1) * NT].bitcast(FP8X4),
+                rhs_scale=w_s[:, g, d * NT : (d + 1) * NT],
+                start=start,
+                stop=stop,
+            )
+
+        def stage2(j):
+            if j in GROUP_FIRST:
+                for g in range(CG):
+                    for i in range(4):
+                        multiply(j, i, g, g == 0, g == CG - 1)
+            else:
+                for i in range(4):
+                    for g in range(CG):
+                        multiply(j, i, g, g == 0, g == CG - 1)
+
+        def finish(j, i):
+            b, m, d = j // 2, 2 * (j % 2) + i // 2, i % 2
             if d == 0:
                 y_tiles[b, m] = outs.tile([P, D], F32, name="y")
             y = y_tiles[b, m]
-            acc = psum.tile([P, NT], F32, name="acc")
-            for g in range(CG):
-                u = b * CG + g
-                nc.tensor.matmul_mx(
-                    out=acc[:],
-                    lhsT=codes[u][:, m * P : (m + 1) * P].bitcast(FP8X4),
-                    lhsT_scale=code_scales[u][:, m * P : (m + 1) * P],
-                    rhs=w_w[:, g, 4 * d * NT : 4 * (d + 1) * NT].bitcast(FP8X4),
-                    rhs_scale=w_s[:, g, d * NT : (d + 1) * NT],
-                    start=(g == 0),
-                    stop=(g == CG - 1),
+            acc = banks[j, i]
+            rows_out = out[b, m * P : (m + 1) * P, :]
+            pieces = 2 if (j, i) == (7, 3) else 1
+            width = NT // pieces
+            for c in range(pieces):
+                cols = slice(d * NT + c * width, d * NT + (c + 1) * width)
+                nc.vector.tensor_tensor(
+                    out=y[:, cols], in0=acc[:, c * width : (c + 1) * width], in1=bias_t[:, cols], op=ADD
                 )
-            cols = slice(d * NT, (d + 1) * NT)
-            if helper:
-                nc.scalar.copy(out=y[:, cols], in_=acc[:])
-                nc.gpsimd.tensor_tensor(out=y[:, cols], in0=y[:, cols], in1=bias_t[:, cols], op=ADD)
-            else:
-                nc.vector.tensor_tensor(out=y[:, cols], in0=acc[:], in1=bias_t[:, cols], op=ADD)
-            if (b, m) == (B - 1, H // P - 1):
-                engine = nc.sync if d == 0 else nc.scalar
-                engine.dma_start(out=out[b, m * P : (m + 1) * P, cols], in_=y[:, cols])
-            elif d == D // NT - 1:
-                nc.sync.dma_start(out=out[b, m * P : (m + 1) * P, :], in_=y[:])
+                if j == 7:
+                    engine = nc.scalar if (i + c) % 2 else nc.sync
+                    engine.dma_start(out=rows_out[:, cols], in_=y[:, cols])
+            if j < 7 and d == D // NT - 1:
+                nc.sync.dma_start(out=rows_out, in_=y[:])
 
         for token in ORDER:
             kind, rest = token.split(":")
@@ -203,6 +247,8 @@ def tile_lag_channel_mixer_s4_kernel(
                     words_t(a[0], a[1])
             elif kind == "S":
                 scales(a[0])
+            elif kind == "SP":
+                scales_packed()
             elif kind == "U":
                 stage1(a[0])
             elif kind == "IV":
@@ -213,7 +259,7 @@ def tile_lag_channel_mixer_s4_kernel(
                 interleave(interleave_g, a[0], a[1])
             elif kind == "Q":
                 quantise(a[0])
-            elif kind == "A":
-                stage2(a[0], a[1], a[2], False)
-            else:
-                stage2(a[0], a[1], a[2], True)
+            elif kind == "H":
+                stage2(a[0])
+            elif kind == "E":
+                finish(a[0], a[1])

from contextlib import ExitStack

import concourse.mybir as mybir

L, H, B, C, D = 1024, 512, 4, 1024, 1024
FLOPS = 2 * L * H * B * C + 2 * B * H * C * D

F32 = mybir.dt.float32
BF16 = mybir.dt.bfloat16
I32 = mybir.dt.int32
U32 = mybir.dt.uint32
U8 = mybir.dt.uint8
FP4X4 = mybir.dt.float4_e2m1fn_x4
FP8X4 = mybir.dt.float8_e4m3fn_x4
ADD = mybir.AluOpType.add
RELU = mybir.ActivationFunctionType.Relu

P = 128
KG = L // 512
CG = C // 512
UNITS = B * CG
NT = 512

ORDER = """
W:0.0 S:0 W:0.1 W:0.2 W:0.3 U:0 W:1 S:1 U:1 W:2 S:2 IV:0.512 S:3 IV:1.256 IS:1.256 Q:0 Q:1 W:3 U:2 IS:2.512
H:0 W:4 SP:0 E:0.0 E:0.1 E:0.2 E:0.3 Q:2 U:3 IS:3.384 H:1 E:1.0 E:1.1 IV:3.128 E:1.2 Q:3 E:1.3 W:5 U:4
IS:4.512 H:2 W:6 E:2.0 E:2.1 E:2.2 E:2.3 Q:4 U:5 IS:5.384 H:3 E:3.0 E:3.1 IV:5.128 E:3.2 Q:5 E:3.3 W:7 U:6
IS:6.512 H:4 E:4.0 E:4.1 E:4.2 E:4.3 Q:6 U:7 IS:7.256 H:5 E:5.0 E:5.1 IV:7.256 E:5.2 Q:7 E:5.3 H:6 E:6.0 E:6.1
E:6.2 E:6.3 H:7 E:7.0 E:7.1 E:7.2 E:7.3
""".split()
GROUP_FIRST = (0, 6)


def tile_lag_channel_mixer_s4_kernel(
    tc, lag_words, lag_scales, x_words, x_scales, w_words, w_scales, level, bias, out
):
    nc = tc.nc
    with ExitStack() as ctx:
        keep = ctx.enter_context(tc.tile_pool(name="keep", bufs=1))
        work = ctx.enter_context(tc.tile_pool(name="work", bufs=3))
        outs = ctx.enter_context(tc.tile_pool(name="outs", bufs=6))
        psum = ctx.enter_context(tc.psum_pool(name="psum", bufs=8))
        ctx.enter_context(tc.manual_schedule())

        lag_w = keep.tile([P, KG, 2 * H], U8, align_bytes=64, name="lag_w")
        lag_s = keep.tile([P, KG, H], U8, align_bytes=64, name="lag_s")
        w_w = keep.tile([P, CG, 4 * D], U8, align_bytes=64, name="w_w")
        w_s = keep.tile([P, CG, D], U8, align_bytes=64, name="w_s")
        lvl = keep.tile([P, UNITS, 4], BF16, align_bytes=64, name="lvl")
        bias_t = keep.tile([P, D], BF16, align_bytes=64, name="bias_t")
        scratch = keep.tile([P, 1], F32, name="scratch")
        x_raw = [keep.tile([P, KG, 1024], U8, align_bytes=64, name="x_raw%d" % u) for u in range(UNITS)]
        x_st = [keep.tile([P, KG, 4, 256], U8, align_bytes=64, name="x_st%d" % u) for u in range(UNITS)]
        xs_raw0 = keep.tile([P, KG, 2 * C], U8, align_bytes=64, name="xs_raw0")
        xs_pk = keep.tile([P, 2 * C], U8, align_bytes=64, name="xs_pk")
        pk_st = keep.tile([P, 2 * CG, 4, P], U8, align_bytes=64, name="pk_st")
        pl1 = keep.tile([P, 2 * CG, 4, P], U8, align_bytes=64, name="pl1")
        xs_st = [keep.tile([P, KG, CG, 4, P], U8, align_bytes=64, name="xs_st%d" % b) for b in range(2)]
        codes = [keep.tile([P, H], U32, align_bytes=64, name="codes%d" % u) for u in range(UNITS)]
        code_scales = [keep.tile([P, H], U8, align_bytes=64, name="cs%d" % u) for u in range(UNITS)]

        def load_x(u, engine=nc.sync):
            src = x_words[:, :, u * 1024 : (u + 1) * 1024].bitcast(I32)
            engine.dma_start(out=x_raw[u][:].bitcast(I32), in_=src.rearrange("k p n -> p k n"))

        def load_scales(engine, dst, src, q):
            rows = src[:, 4 * q : 4 * q + 4, :].bitcast(I32)
            engine.dma_start(out=dst[32 * q : 32 * q + 4].bitcast(I32), in_=rows.rearrange("k r n -> r k n"))

        nc.vector.memset(lag_s[:].rearrange("p k n -> p (k n)").bitcast(I32), 0)
        nc.vector.memset(xs_raw0[:].rearrange("p k n -> p (k n)").bitcast(I32), 0)
        nc.vector.memset(codes[UNITS - 1][:], 0)
        nc.vector.memset(code_scales[UNITS - 1][:].bitcast(I32), 0)
        nc.vector.memset(scratch[:], 0.0)
        load_x(0)
        nc.gpsimd.dma_start(out=lag_w[:].bitcast(I32), in_=lag_words[:, :, :].bitcast(I32).rearrange("k p n -> p k n"))
        for q in range(4):
            load_scales(nc.scalar if q < 3 else nc.gpsimd, lag_s, lag_scales, q)
            load_scales(nc.sync, xs_raw0, x_scales[:, :, 0 : 2 * C], q)
        nc.gpsimd.memset(xs_pk[:].bitcast(I32), 0)
        nc.gpsimd.memset(pl1[:].rearrange("p a t m -> p (a t m)").bitcast(I32), 0)
        nc.gpsimd.memset(w_s[:].rearrange("p k n -> p (k n)").bitcast(I32), 0)
        nc.scalar.activation(out=scratch[:], in_=scratch[:], func=RELU)
        nc.scalar.dma_start(out=lvl[:], in_=level.rearrange("b (g p t) -> p (b g) t", g=CG, t=4))
        load_x(1)
        load_x(2)
        for q in range(4):
            nc.sync.dma_start(
                out=xs_pk[32 * q : 32 * q + 8, :].bitcast(I32),
                in_=x_scales[:, 4 * q : 4 * q + 4, 2 * C : 4 * C].bitcast(I32),
            )
        for q in range(4):
            load_scales(nc.sync, w_s, w_scales, q)
        load_x(3)
        for g in range(CG):
            nc.sync.dma_start(
                out=w_w[:, g, :].bitcast(I32),
                in_=w_words[g].rearrange("p n t -> p (n t)").bitcast(I32),
            )
        load_x(4)
        nc.sync.dma_start(out=bias_t[:], in_=bias.partition_broadcast(P))
        for u in range(5, UNITS):
            load_x(u)
        warm = psum.tile([P, NT], F32, name="acc")
        for i in range(6):
            nc.tensor.matmul_mx(
                out=warm[:],
                lhsT=codes[UNITS - 1][:, 0:P].bitcast(FP8X4),
                lhsT_scale=code_scales[UNITS - 1][:, 0:P],
                rhs=codes[UNITS - 1][:].bitcast(FP8X4),
                rhs_scale=code_scales[UNITS - 1][:],
                start=True,
                stop=True,
            )

        def words(u):
            nc.vector.tensor_copy(
                out=x_st[u][:].rearrange("p k t (m b) -> p k t m b", b=2),
                in_=x_raw[u][:].rearrange("p k (m t b) -> p k t m b", t=4, b=2),
            )

        def words_t(u, t):
            nc.vector.tensor_copy(
                out=x_st[u][:, :, t, :].rearrange("p k (m b) -> p k m b", b=2),
                in_=x_raw[u][:].rearrange("p k (m t b) -> p k t m b", t=4, b=2)[:, :, t],
            )

        def scales(u):
            b, g = divmod(u, CG)
            nc.vector.tensor_copy(
                out=xs_st[b][:, :, g], in_=xs_raw0[:, :, u * 512 : (u + 1) * 512].rearrange("p k (m t) -> p k t m", t=4)
            )

        def scales_packed():
            nc.vector.tensor_copy(out=pk_st[:], in_=xs_pk[:].rearrange("p (a m t) -> p a t m", t=4, m=P))
            for q in range(4):
                nc.sync.dma_start(
                    out=pl1[32 * q : 32 * q + 4].bitcast(I32), in_=pk_st[32 * q + 4 : 32 * q + 8].bitcast(I32)
                )

        def x_scale(u, k, t):
            if u < 2 * CG:
                return xs_st[u // CG][:, k, u % CG, t, :]
            return (pk_st, pl1)[k][:, u - 2 * CG, t, :]

        rows = {}
        inter = {}

        def stage1(u):
            rows[u] = work.tile([P, 4, H], BF16, align_bytes=64, name="rows")
            for t in range(4):
                acc = psum.tile([P, NT], F32, name="acc")
                for k in range(KG):
                    nc.tensor.matmul_mx(
                        out=acc[:],
                        lhsT=x_st[u][:, k, t, :].bitcast(FP4X4),
                        lhsT_scale=x_scale(u, k, t),
                        rhs=lag_w[:, k, :].bitcast(FP4X4),
                        rhs_scale=lag_s[:, k, :],
                        start=(k == 0),
                        stop=(k == KG - 1),
                    )
                nc.scalar.activation(
                    out=rows[u][:, t, :], in_=acc[:], func=RELU, bias=lvl[:, u, t : t + 1]
                )

        def get_inter(u):
            if u not in inter:
                inter[u] = work.tile([P, H, 4], BF16, align_bytes=64, name="inter")
            return inter[u]

        filled = {}

        def interleave(engine_copy, u, n):
            n0 = filled.get(u, 0)
            filled[u] = n0 + n
            engine_copy(
                out=get_inter(u)[:, n0 : n0 + n, :].rearrange("p (c i) t -> p c t i", i=4),
                in_=rows[u][:, :, n0 : n0 + n].rearrange("p t (c i) -> p c t i", i=4),
            )

        def interleave_g(out, in_):
            nc.gpsimd.tensor_scalar(out=out, in0=in_, scalar1=1.0, scalar2=0.0, op0=mybir.AluOpType.mult, op1=ADD)

        def quantise(u):
            nc.vector.quantize_mx(
                out=codes[u][:].bitcast(FP8X4),
                scales=code_scales[u][:],
                in_=inter[u][:].rearrange("p n t -> p (n t)"),
            )

        y_tiles = {}
        banks = {}

        def multiply(j, i, g, start, stop):
            u = (j // 2) * CG + g
            m, d = 2 * (j % 2) + i // 2, i % 2
            if start:
                banks[j, i] = psum.tile([P, NT], F32, name="acc")
            nc.tensor.matmul_mx(
                out=banks[j, i][:],
                lhsT=codes[u][:, m * P : (m + 1) * P].bitcast(FP8X4),
                lhsT_scale=code_scales[u][:, m * P : (m + 1) * P],
                rhs=w_w[:, g, 4 * d * NT : 4 * (d + 1) * NT].bitcast(FP8X4),
                rhs_scale=w_s[:, g, d * NT : (d + 1) * NT],
                start=start,
                stop=stop,
            )

        def stage2(j):
            if j in GROUP_FIRST:
                for g in range(CG):
                    for i in range(4):
                        multiply(j, i, g, g == 0, g == CG - 1)
            else:
                for i in range(4):
                    for g in range(CG):
                        multiply(j, i, g, g == 0, g == CG - 1)

        def finish(j, i):
            b, m, d = j // 2, 2 * (j % 2) + i // 2, i % 2
            if d == 0:
                y_tiles[b, m] = outs.tile([P, D], F32, name="y")
            y = y_tiles[b, m]
            acc = banks[j, i]
            rows_out = out[b, m * P : (m + 1) * P, :]
            pieces = 2 if (j, i) == (7, 3) else 1
            width = NT // pieces
            for c in range(pieces):
                cols = slice(d * NT + c * width, d * NT + (c + 1) * width)
                nc.vector.tensor_tensor(
                    out=y[:, cols], in0=acc[:, c * width : (c + 1) * width], in1=bias_t[:, cols], op=ADD
                )
                if j == 7:
                    engine = nc.scalar if (i + c) % 2 else nc.sync
                    engine.dma_start(out=rows_out[:, cols], in_=y[:, cols])
            if j < 7 and d == D // NT - 1:
                nc.sync.dma_start(out=rows_out, in_=y[:])

        for token in ORDER:
            kind, rest = token.split(":")
            a = [int(v) for v in rest.split(".")]
            if kind == "W":
                if len(a) == 1:
                    words(a[0])
                else:
                    words_t(a[0], a[1])
            elif kind == "S":
                scales(a[0])
            elif kind == "SP":
                scales_packed()
            elif kind == "U":
                stage1(a[0])
            elif kind == "IV":
                interleave(nc.vector.tensor_copy, a[0], a[1])
            elif kind == "IS":
                interleave(nc.scalar.copy, a[0], a[1])
            elif kind == "IG":
                interleave(interleave_g, a[0], a[1])
            elif kind == "Q":
                quantise(a[0])
            elif kind == "H":
                stage2(a[0])
            elif kind == "E":
                finish(a[0], a[1])
